import numpy as np
import ml_dtypes


def mxq(x, axis, fmt="e4m3"):
    dtype, down = {"e4m3": (ml_dtypes.float8_e4m3fn, 7), "e5m2": (ml_dtypes.float8_e5m2, 14)}[fmt]
    v = np.moveaxis(np.asarray(x, np.float32).astype(ml_dtypes.bfloat16).astype(np.float64), axis, -1)
    blocks = v.reshape(v.shape[:-1] + (-1, 32))
    amax = np.abs(blocks).max(-1, keepdims=True)
    byte = np.maximum(np.where(amax > 0, np.frexp(amax)[1] - 1 + 127, 0) - down, 1)
    scale = np.exp2(byte - 127.0)
    codes = (blocks / scale).astype(np.float32).astype(dtype).astype(np.float64)
    return np.moveaxis((codes * scale).reshape(v.shape), -1, axis)


WIDE = False


def mx_kscale(k):
    if not WIDE:
        return np.ones(k)
    levels = np.array([10, -10, 5, -5, 0])
    if k % 512:
        return np.exp2(np.random.permutation(np.resize(levels, k // 32))).repeat(32)
    a = np.empty((k // 512, 16))
    for p in range(k // 512):
        a[p, :8] = np.random.permutation(np.resize(levels, 8))
        for g in range(8):
            far = levels[np.abs(levels - a[p, g]) >= 10]
            a[p, g + 8] = far[np.random.randint(len(far))]
    return np.exp2(a.ravel()).repeat(32)


def f64(x):
    return np.asarray(x).astype(np.float64)


def striped(idx):
    return np.tile(idx.reshape(-1, 16).T, (8, 1)).astype(np.uint16)


def unstriped(offs):
    return offs[:16].T.reshape(-1).astype(np.int64)


E2M1 = np.array([0.0, 0.5, 1.0, 1.5, 2.0, 3.0, 4.0, 6.0, -0.0, -0.5, -1.0, -1.5, -2.0, -3.0, -4.0, -6.0])


def pack_weight(w, fmt):
    k, n = w.shape
    w = f64(np.asarray(w, np.float32).astype(ml_dtypes.bfloat16)).reshape(k // 32, 32, n)
    amax = np.abs(w).max(1)
    if fmt == "e4m3":
        byte = np.frexp(amax)[1] - 1 + 127 - 7
    else:
        mant, ex = np.frexp(amax / 6.0)
        byte = np.where(mant > 0.5, ex, ex - 1) + 127
    byte = np.clip(np.where(amax > 0, byte, 1), 1, 254)
    scaled = (w * np.exp2(127.0 - byte)[:, None, :]).reshape(k, n).astype(np.float32)
    by_word = np.ascontiguousarray(scaled.reshape(k // 512, 128, 4, n).transpose(0, 1, 3, 2))
    if fmt == "e4m3":
        words = by_word.astype(ml_dtypes.float8_e4m3fn).view(np.uint8)
    else:
        c = by_word.astype(ml_dtypes.float4_e2m1fn).view(np.uint8) & 0xF
        words = (c[..., 0::2] | (c[..., 1::2] << 4)).reshape(k // 512, 128, 2 * n)
    return np.ascontiguousarray(words), np.ascontiguousarray(byte.astype(np.uint8).reshape(k // 512, 16, n))


def unpack_weight(words, scales, fmt):
    g, _, n = scales.shape
    words = np.ascontiguousarray(words).reshape(g, 128, n, -1)
    if fmt == "e4m3":
        vals = words.view(ml_dtypes.float8_e4m3fn).astype(np.float64)
    else:
        nib = np.empty((g, 128, n, 4), np.uint8)
        nib[..., 0::2] = words & 0xF
        nib[..., 1::2] = words >> 4
        vals = E2M1[nib]
    vals = vals * np.repeat(np.exp2(scales.astype(np.float64) - 127.0), 8, axis=1)[..., None]
    return vals.transpose(0, 1, 3, 2).reshape(g * 512, n)


def gelu(v):
    return 0.5 * v * (1.0 + np.tanh(np.sqrt(2.0 / np.pi) * (v + 0.044715 * v**3)))


T, S, K, K2, H, N = 4096, 1024, 1024, 512, 1024, 512


def setup_inputs():
    n = np.random.standard_normal
    s = mx_kscale(K)[:, None]
    s2 = mx_kscale(K2)[:, None]
    u = mx_kscale(H)[:, None]
    d = {}
    d["tab_words"], d["tab_scales"] = pack_weight(n((K, T)) * s, "e4m3")
    d["offs"] = striped(np.random.permutation(T)[:S])
    d["xs_words"], d["xs_scales"] = pack_weight(n((K2, S)) * s2, "e4m3")
    d["w1"] = (n((K, H)) / s / K ** 0.5).astype(np.float32)
    d["w2_words"], d["w2_scales"] = pack_weight(n((K2, H)) / s2 / K2 ** 0.5, "e2m1")
    d["gain"] = (np.exp(0.3 * n(H)) * u[:, 0]).astype(np.float32)
    d["w3"] = (1.5 * n((H, N)) / u / H ** 0.5).astype(np.float32)
    d["w4_words"], d["w4_scales"] = pack_weight(2.0 * n((H, N)) / u / H ** 0.5, "e4m3")
    return d


def reference(tab_words, tab_scales, offs, xs_words, xs_scales, w1, w2_words, w2_scales,
              gain, w3, w4_words, w4_scales):
    v = unpack_weight(tab_words, tab_scales, "e4m3")[:, unstriped(offs)]
    xs = unpack_weight(xs_words, xs_scales, "e4m3")
    w2 = unpack_weight(w2_words, w2_scales, "e2m1")
    w4 = unpack_weight(w4_words, w4_scales, "e4m3")
    both = mxq(f64(w1), 0, "e4m3").T @ v + w2.T @ xs
    h = f64(gain)[:, None] * np.tanh(both)
    hq = mxq(h, 0, "e4m3")
    feed = mxq(f64(w3), 0, "e4m3").T @ hq
    damp = w4.T @ hq
    return feed / np.sqrt(1.0 + np.square(damp))

@@ -1,0 +1,254 @@
+from contextlib import ExitStack
+
+import concourse.mybir as mybir
+
+T, S, K, K2, H, N = 4096, 1024, 1024, 512, 1024, 512
+FLOPS = 2 * S * (K * H + K2 * H + 2 * H * N)
+
+F32 = mybir.dt.float32
+BF16 = mybir.dt.bfloat16
+I32 = mybir.dt.int32
+U32 = mybir.dt.uint32
+U16 = mybir.dt.uint16
+U8 = mybir.dt.uint8
+FP8X4 = mybir.dt.float8_e4m3fn_x4
+FP4X4 = mybir.dt.float4_e2m1fn_x4
+ACT = mybir.ActivationFunctionType
+MULT = mybir.AluOpType.mult
+
+P = 128
+PACK = 4
+KP = P * PACK
+UNIT = 128
+HALF = 512
+
+
+def tile_list_oil_feed_scores_kernel(tc, tab_words, tab_scales, offs, xs_words, xs_scales, w1, w2_words,
+                                               w2_scales, gain, w3, w4_words, w4_scales, out):
+    nc = tc.nc
+    with ExitStack() as ctx:
+        keep = ctx.enter_context(tc.tile_pool(name="keep", bufs=1))
+        cast_pool = ctx.enter_context(tc.tile_pool(name="cast", bufs=6))
+        tanh_pool = ctx.enter_context(tc.tile_pool(name="tanh", bufs=8))
+        sq_pool = ctx.enter_context(tc.tile_pool(name="sq", bufs=4))
+        damp_pool = ctx.enter_context(tc.tile_pool(name="damping", bufs=8))
+        out_pool = ctx.enter_context(tc.tile_pool(name="result", bufs=4))
+        psum = ctx.enter_context(tc.psum_pool(name="psum", bufs=8))
+
+        def kept(shape, dtype, name):
+            return keep.tile(shape, dtype, name=name, align_bytes=64)
+
+        offsets = keep.tile([P, S // 16], U16, name="offsets")
+        tab_w = [kept([P, T], U32, "tab_w%d" % a) for a in range(2)]
+        tab_s = kept([P, T], U8, "tab_s")
+        v_w = [kept([P, S], U32, "v_w%d" % a) for a in range(2)]
+        v_s = kept([P, S], U8, "v_s")
+        xs_w = kept([P, S], U32, "xs_w")
+        xs_s = kept([P, S], U8, "xs_s")
+        w2_w_raw = kept([P, 2 * H], U8, "w2_w_raw")
+        w2_s_raw = kept([P, H], U8, "w2_s_raw")
+        w2_w = kept([P, 2 * H], U8, "w2_w")
+        w2_s = kept([P, H], U8, "w2_s")
+        w4_w = kept([P, 2, N], U32, "w4_w")
+        w4_s = kept([P, N], U8, "w4_s")
+        gains = kept([P, 2, PACK], F32, "gains")
+        w1_raw = {(a, b): kept([P, PACK, KP], F32, "w1_raw%d%d" % (a, b)) for a in range(2) for b in range(2)}
+        w1_w = {(a, b): kept([P, KP], U32, "w1_w%d%d" % (a, b)) for a in range(2) for b in range(2)}
+        w1_s = {(a, b): kept([P, KP], U8, "w1_s%d%d" % (a, b)) for a in range(2) for b in range(2)}
+        w3_raw = [kept([P, PACK, N], F32, "w3_raw%d" % b) for b in range(2)]
+        w3_w = [kept([P, N], U32, "w3_w%d" % b) for b in range(2)]
+        w3_s = [kept([P, N], U8, "w3_s%d" % b) for b in range(2)]
+        h_w = {(b, g): kept([P, HALF], U32, "h_w%d%d" % (b, g)) for b in range(2) for g in range(2)}
+        h_s = {(b, g): kept([P, HALF], U8, "h_s%d%d" % (b, g)) for b in range(2) for g in range(2)}
+
+        h_bf = [kept([P, 2 * UNIT * PACK], BF16, "h_bf%d" % i) for i in range(2)]
+
+        def load_words(dst, src):
+            nc.sync.dma_start(out=dst.bitcast(I32), in_=src.rearrange("p n t -> p (n t)").bitcast(I32))
+
+        def load_scales(queue, dst, src):
+            rows = 4 * src.shape[0]
+            for q in range(4):
+                queue.dma_start(out=dst[32 * q : 32 * q + rows, :].bitcast(I32),
+                                in_=src[:, 4 * q : 4 * q + 4, :].bitcast(I32))
+
+        def load_w1(a, b):
+            rows = w1[a * KP : (a + 1) * KP, b * KP : (b + 1) * KP]
+            nc.sync.dma_start(out=w1_raw[a, b][:], in_=rows.rearrange("(p j) c -> p j c", j=PACK))
+
+        nc.vector.memset(tab_s[:].bitcast(I32), 0)
+        nc.vector.memset(w4_s[:].bitcast(I32), 0)
+        nc.gpsimd.memset(w2_s_raw[:].bitcast(I32), 0)
+        nc.gpsimd.memset(xs_s[:].bitcast(I32), 0)
+
+        load_words(tab_w[0][:, : T // 2], tab_words[0, :, : T // 2, :])
+        nc.sync.dma_start(offsets[:], offs)
+        nc.sync.dma_start(out=gains[:], in_=gain.rearrange("(b p t) -> p b t", b=2, t=PACK))
+        load_scales(nc.sync, tab_s, tab_scales)
+        load_words(tab_w[0][:, T // 2 :], tab_words[0, :, T // 2 :, :])
+        nc.sync.dma_start(out=w2_w_raw[:].bitcast(I32), in_=w2_words[0].bitcast(I32))
+        load_scales(nc.sync, w2_s_raw, w2_scales)
+        load_words(xs_w[:], xs_words[0])
+        load_w1(0, 0)
+        load_scales(nc.sync, xs_s, xs_scales)
+        load_words(tab_w[1][:], tab_words[1])
+        load_w1(1, 0)
+        load_w1(0, 1)
+        load_w1(1, 1)
+        nc.sync.dma_start(out=w4_w[:].bitcast(I32), in_=w4_words.rearrange("b p n t -> p b (n t)").bitcast(I32))
+        load_scales(nc.sync, w4_s, w4_scales)
+        for b in range(2):
+            nc.sync.dma_start(out=w3_raw[b][:], in_=w3[b * KP : (b + 1) * KP, :].rearrange("(p j) c -> p j c", j=PACK))
+
+        def cast(on_scalar, dst, src):
+            if on_scalar:
+                nc.scalar.activation(out=dst, in_=src, func=ACT.Copy)
+            else:
+                nc.vector.tensor_copy(out=dst, in_=src)
+
+        def cast_w1(a, b, t0, t1, on_scalar):
+            staged = cast_pool.tile([P, (t1 - t0) * KP], BF16, name="staged", align_bytes=64)
+            src = w1_raw[a, b][:].rearrange("p j (m t) -> p m j t", t=PACK)[:, :, :, t0:t1]
+            cast(on_scalar, staged[:].rearrange("p (t m j) -> p m j t", m=P, j=PACK), src)
+            return (staged, w1_w[a, b][:, t0 * P : t1 * P], w1_s[a, b][:, t0 * P : t1 * P])
+
+        def cast_w3(b, c0, c1, on_scalar):
+            staged = cast_pool.tile([P, (c1 - c0) * PACK], BF16, name="staged", align_bytes=64)
+            src = w3_raw[b][:, :, c0:c1].rearrange("p j (c i) -> p c j i", i=4)
+            cast(on_scalar, staged[:].rearrange("p (c i j) -> p c j i", i=4, j=PACK), src)
+            return (staged, w3_w[b][:, c0:c1], w3_s[b][:, c0:c1])
+
+        def quantize(job):
+            staged, words, scales = job
+            nc.vector.quantize_mx(out=words.bitcast(FP8X4), scales=scales, in_=staged[:])
+
+        def stream_pass(bank, b, u, start, stop):
+            cols = slice(u * UNIT, (u + 1) * UNIT)
+            for t in range(PACK):
+                c0 = b * KP + t * P
+                nc.tensor.matmul_mx(
+                    out=bank[:, t * UNIT : (t + 1) * UNIT],
+                    lhsT=w2_w[:, 2 * c0 : 2 * (c0 + P)].bitcast(FP4X4), lhsT_scale=w2_s[:, c0 : c0 + P],
+                    rhs=xs_w[:, cols].bitcast(FP8X4), rhs_scale=xs_s[:, cols],
+                    start=start and t == 0, stop=stop and t == PACK - 1)
+
+        def table_pass(bank, a, b, u, start, stop):
+            cols = slice(u * UNIT, (u + 1) * UNIT)
+            for t in range(PACK):
+                wcols = slice(t * P, (t + 1) * P)
+                nc.tensor.matmul_mx(
+                    out=bank[:, t * UNIT : (t + 1) * UNIT],
+                    lhsT=w1_w[a, b][:, wcols].bitcast(FP8X4), lhsT_scale=w1_s[a, b][:, wcols],
+                    rhs=v_w[a][:, cols].bitcast(FP8X4), rhs_scale=v_s[4 * a : P, cols],
+                    start=start and t == 0, stop=stop and t == PACK - 1)
+
+        units = range(S // UNIT)
+        nc.vector.tensor_copy(v_w[0][:], tab_w[0][:].indirect(offsets[:]))
+        nc.vector.tensor_copy(out=w2_w[:].rearrange("p (b t m e) -> p b m t e", b=2, t=PACK, e=2),
+                              in_=w2_w_raw[:].rearrange("p (b m t e) -> p b m t e", b=2, t=PACK, e=2))
+        nc.vector.tensor_copy(out=w2_s[:].rearrange("p (b t m) -> p b m t", b=2, t=PACK),
+                              in_=w2_s_raw[:].rearrange("p (b m t) -> p b m t", b=2, t=PACK))
+        nc.vector.tensor_copy(v_s[:], tab_s[:].indirect(offsets[:]))
+        quantize(cast_w1(0, 0, 0, 4, True))
+        nc.vector.tensor_copy(v_w[1][:], tab_w[1][:].indirect(offsets[:]))
+        low = cast_w1(1, 0, 0, 2, True)
+        high = cast_w1(1, 0, 2, 4, False)
+        quantize(low)
+        quantize(high)
+        quantize(cast_w1(0, 1, 0, 4, False))
+        quantize(cast_w1(1, 1, 0, 4, False))
+
+        tanhs = {}
+
+        def squash(bank, b, u):
+            if u % 2 == 0:
+                tanhs[b, u // 2] = tanh_pool.tile([P, 2, UNIT, PACK], F32, name="tanh")
+            nc.scalar.activation(out=tanhs[b, u // 2][:, u % 2, :, :],
+                                 in_=bank[:].rearrange("p (t n) -> p n t", t=PACK), func=ACT.Tanh)
+
+        def first_hidden_half():
+            banks = [psum.tile([P, PACK * UNIT], F32, name="bank") for u in units]
+            for u in units:
+                stream_pass(banks[u], 0, u, True, False)
+            for u in units:
+                table_pass(banks[u], 0, 0, u, False, False)
+            for u in units:
+                table_pass(banks[u], 1, 0, u, False, True)
+                squash(banks[u], 0, u)
+
+        def second_hidden_half():
+            for u in units:
+                bank = psum.tile([P, PACK * UNIT], F32, name="bank")
+                stream_pass(bank, 1, u, True, False)
+                table_pass(bank, 0, 1, u, False, False)
+                table_pass(bank, 1, 1, u, False, True)
+                squash(bank, 1, u)
+
+        def apply_gain(b, pair):
+            h = h_bf[pair % 2]
+            h_view = h[:].rearrange("p (u n t) -> p u n t", u=2, t=PACK)
+            for i in range(2):
+                nc.vector.tensor_tensor(out=h_view[:, i, :, :], in0=tanhs[b, pair][:, i, :, :],
+                                        in1=gains[:, b : b + 1, :].broadcast_to([P, UNIT, PACK]), op=MULT)
+            g, cols = pair // 2, slice((pair % 2) * 2 * UNIT, (pair % 2 + 1) * 2 * UNIT)
+            return (h, h_w[b, g][:, cols], h_s[b, g][:, cols])
+
+        def readout(words, scales, g):
+            banks = []
+            for i in range(N // P):
+                bank = psum.tile([P, HALF], F32, name="bank")
+                cols = slice(i * P, (i + 1) * P)
+                for b in range(2):
+                    nc.tensor.matmul_mx(
+                        out=bank[:], lhsT=words(b, cols).bitcast(FP8X4), lhsT_scale=scales(b, cols),
+                        rhs=h_w[b, g][:].bitcast(FP8X4), rhs_scale=h_s[b, g][:], start=b == 0, stop=b == 1)
+                banks.append(bank)
+            return banks
+
+        def pieces(g, i):
+            last = g == 1 and i == N // P - 1
+            return [slice(0, HALF // 2), slice(HALF // 2, HALF)] if last else [slice(0, HALF)]
+
+        def damping(g):
+            banks = readout(lambda b, cols: w4_w[:, b, cols], lambda b, cols: w4_s[4 * b : P, cols], g)
+            factors = []
+            for i, bank in enumerate(banks):
+                square = sq_pool.tile([P, HALF], F32, name="square")
+                factor = damp_pool.tile([P, HALF], F32, name="factor")
+                for cols in pieces(g, i):
+                    nc.scalar.activation(out=square[:, cols], in_=bank[:, cols], func=ACT.Square)
+                for cols in pieces(g, i):
+                    nc.scalar.activation(out=factor[:, cols], in_=square[:, cols], func=ACT.Abs_reciprocal_sqrt,
+                                         bias=1.0)
+                factors.append(factor)
+            return factors
+
+        def feed(g, factors):
+            banks = readout(lambda b, cols: w3_w[b][:, cols], lambda b, cols: w3_s[b][:, cols], g)
+            for i, bank in enumerate(banks):
+                result = out_pool.tile([P, HALF], F32, name="result")
+                rows = out[i * P : (i + 1) * P, g * HALF : (g + 1) * HALF]
+                for cols in pieces(g, i):
+                    nc.vector.tensor_tensor(out=result[:, cols], in0=bank[:, cols], in1=factors[i][:, cols], op=MULT)
+                    nc.sync.dma_start(out=rows[:, cols], in_=result[:, cols])
+
+        first_hidden_half()
+        second_hidden_half()
+        pending = None
+        factors = {}
+        for g in range(2):
+            for b in range(2):
+                for pair in (2 * g, 2 * g + 1):
+                    job = apply_gain(b, pair)
+                    if pending is not None:
+                        quantize(pending)
+                    pending = job
+            if g == 1:
+                quantize(pending)
+        w3_jobs = [cast_w3(b, c0, c0 + 256, b == 0) for b in range(2) for c0 in (0, 256)]
+        for job in w3_jobs:
+            quantize(job)
+        factors[0] = damping(0)
+        factors[1] = damping(1)
+        feed(0, factors[0])
+        feed(1, factors[1])

@@ -28,11 +28,11 @@ def tile_list_oil_feed_scores_kernel(tc, tab_words, tab_scales, offs, xs_words, 
     nc = tc.nc
     with ExitStack() as ctx:
         keep = ctx.enter_context(tc.tile_pool(name="keep", bufs=1))
-        cast_pool = ctx.enter_context(tc.tile_pool(name="cast", bufs=6))
+        cast_pool = ctx.enter_context(tc.tile_pool(name="cast", bufs=5))
         tanh_pool = ctx.enter_context(tc.tile_pool(name="tanh", bufs=8))
         sq_pool = ctx.enter_context(tc.tile_pool(name="sq", bufs=4))
         damp_pool = ctx.enter_context(tc.tile_pool(name="damping", bufs=8))
-        out_pool = ctx.enter_context(tc.tile_pool(name="result", bufs=4))
+        out_pool = ctx.enter_context(tc.tile_pool(name="result", bufs=8))
         psum = ctx.enter_context(tc.psum_pool(name="psum", bufs=8))
 
         def kept(shape, dtype, name):
@@ -61,7 +61,7 @@ def tile_list_oil_feed_scores_kernel(tc, tab_words, tab_scales, offs, xs_words, 
         h_w = {(b, g): kept([P, HALF], U32, "h_w%d%d" % (b, g)) for b in range(2) for g in range(2)}
         h_s = {(b, g): kept([P, HALF], U8, "h_s%d%d" % (b, g)) for b in range(2) for g in range(2)}
 
-        h_bf = [kept([P, 2 * UNIT * PACK], BF16, "h_bf%d" % i) for i in range(2)]
+        h_bf = [kept([P, 2 * UNIT * PACK], BF16, "h_bf%d" % i) for i in range(3)]
 
         def load_words(dst, src):
             nc.sync.dma_start(out=dst.bitcast(I32), in_=src.rearrange("p n t -> p (n t)").bitcast(I32))
@@ -77,19 +77,19 @@ def tile_list_oil_feed_scores_kernel(tc, tab_words, tab_scales, offs, xs_words, 
             nc.sync.dma_start(out=w1_raw[a, b][:], in_=rows.rearrange("(p j) c -> p j c", j=PACK))
 
         nc.vector.memset(tab_s[:].bitcast(I32), 0)
+        nc.vector.memset(w2_s_raw[:].bitcast(I32), 0)
+        nc.vector.memset(xs_s[:].bitcast(I32), 0)
         nc.vector.memset(w4_s[:].bitcast(I32), 0)
-        nc.gpsimd.memset(w2_s_raw[:].bitcast(I32), 0)
-        nc.gpsimd.memset(xs_s[:].bitcast(I32), 0)
 
-        load_words(tab_w[0][:, : T // 2], tab_words[0, :, : T // 2, :])
+        load_scales(nc.gpsimd, tab_s, tab_scales)
+        nc.gpsimd.dma_start(out=gains[:], in_=gain.rearrange("(b p t) -> p b t", b=2, t=PACK))
+
         nc.sync.dma_start(offsets[:], offs)
-        nc.sync.dma_start(out=gains[:], in_=gain.rearrange("(b p t) -> p b t", b=2, t=PACK))
-        load_scales(nc.sync, tab_s, tab_scales)
-        load_words(tab_w[0][:, T // 2 :], tab_words[0, :, T // 2 :, :])
+        load_words(tab_w[0][:], tab_words[0])
         nc.sync.dma_start(out=w2_w_raw[:].bitcast(I32), in_=w2_words[0].bitcast(I32))
         load_scales(nc.sync, w2_s_raw, w2_scales)
-        load_words(xs_w[:], xs_words[0])
         load_w1(0, 0)
+        load_words(xs_w[:], xs_words[0])
         load_scales(nc.sync, xs_s, xs_scales)
         load_words(tab_w[1][:], tab_words[1])
         load_w1(1, 0)
@@ -142,19 +142,19 @@ def tile_list_oil_feed_scores_kernel(tc, tab_words, tab_scales, offs, xs_words, 
                     rhs=v_w[a][:, cols].bitcast(FP8X4), rhs_scale=v_s[4 * a : P, cols],
                     start=start and t == 0, stop=stop and t == PACK - 1)
 
-        units = range(S // UNIT)
+        units = list(range(S // UNIT))
         nc.vector.tensor_copy(v_w[0][:], tab_w[0][:].indirect(offsets[:]))
-        nc.vector.tensor_copy(out=w2_w[:].rearrange("p (b t m e) -> p b m t e", b=2, t=PACK, e=2),
-                              in_=w2_w_raw[:].rearrange("p (b m t e) -> p b m t e", b=2, t=PACK, e=2))
-        nc.vector.tensor_copy(out=w2_s[:].rearrange("p (b t m) -> p b m t", b=2, t=PACK),
-                              in_=w2_s_raw[:].rearrange("p (b m t) -> p b m t", b=2, t=PACK))
+        nc.vector.tensor_copy(out=w2_w[:].rearrange("p (b t m e) -> p b t m e", b=2, t=PACK, e=2),
+                              in_=w2_w_raw[:].rearrange("p (b m t e) -> p b t m e", b=2, t=PACK, e=2))
+        nc.vector.tensor_copy(out=w2_s[:].rearrange("p (b t m) -> p b t m", b=2, t=PACK),
+                              in_=w2_s_raw[:].rearrange("p (b m t) -> p b t m", b=2, t=PACK))
         nc.vector.tensor_copy(v_s[:], tab_s[:].indirect(offsets[:]))
         quantize(cast_w1(0, 0, 0, 4, True))
         nc.vector.tensor_copy(v_w[1][:], tab_w[1][:].indirect(offsets[:]))
         low = cast_w1(1, 0, 0, 2, True)
         high = cast_w1(1, 0, 2, 4, False)
-        quantize(low)
         quantize(high)
+        quantize(low)
         quantize(cast_w1(0, 1, 0, 4, False))
         quantize(cast_w1(1, 1, 0, 4, False))
 
@@ -184,12 +184,10 @@ def tile_list_oil_feed_scores_kernel(tc, tab_words, tab_scales, offs, xs_words, 
                 table_pass(bank, 1, 1, u, False, True)
                 squash(bank, 1, u)
 
-        def apply_gain(b, pair):
-            h = h_bf[pair % 2]
-            h_view = h[:].rearrange("p (u n t) -> p u n t", u=2, t=PACK)
-            for i in range(2):
-                nc.vector.tensor_tensor(out=h_view[:, i, :, :], in0=tanhs[b, pair][:, i, :, :],
-                                        in1=gains[:, b : b + 1, :].broadcast_to([P, UNIT, PACK]), op=MULT)
+        def apply_gain(b, pair, h):
+            nc.vector.tensor_tensor(out=h[:].rearrange("p (n t) -> p n t", t=PACK),
+                                    in0=tanhs[b, pair][:].rearrange("p u n t -> p (u n) t"),
+                                    in1=gains[:, b : b + 1, :].broadcast_to([P, 2 * UNIT, PACK]), op=MULT)
             g, cols = pair // 2, slice((pair % 2) * 2 * UNIT, (pair % 2 + 1) * 2 * UNIT)
             return (h, h_w[b, g][:, cols], h_s[b, g][:, cols])
 
@@ -239,13 +237,13 @@ def tile_list_oil_feed_scores_kernel(tc, tab_words, tab_scales, offs, xs_words, 
         for g in range(2):
             for b in range(2):
                 for pair in (2 * g, 2 * g + 1):
-                    job = apply_gain(b, pair)
+                    job = apply_gain(b, pair, h_bf[(4 * g + 2 * b + pair % 2) % 3])
                     if pending is not None:
                         quantize(pending)
                     pending = job
             if g == 1:
                 quantize(pending)
-        w3_jobs = [cast_w3(b, c0, c0 + 256, b == 0) for b in range(2) for c0 in (0, 256)]
+        w3_jobs = [cast_w3(b, c0, c0 + 256, b == 0 and c0 == 0) for b in range(2) for c0 in (0, 256)]
         for job in w3_jobs:
             quantize(job)
         factors[0] = damping(0)

@@ -28,11 +28,11 @@ def tile_list_oil_feed_scores_kernel(tc, tab_words, tab_scales, offs, xs_words, 
     nc = tc.nc
     with ExitStack() as ctx:
         keep = ctx.enter_context(tc.tile_pool(name="keep", bufs=1))
-        cast_pool = ctx.enter_context(tc.tile_pool(name="cast", bufs=5))
+        cast_pool = ctx.enter_context(tc.tile_pool(name="cast", bufs=3))
         tanh_pool = ctx.enter_context(tc.tile_pool(name="tanh", bufs=8))
         sq_pool = ctx.enter_context(tc.tile_pool(name="sq", bufs=4))
         damp_pool = ctx.enter_context(tc.tile_pool(name="damping", bufs=8))
-        out_pool = ctx.enter_context(tc.tile_pool(name="result", bufs=8))
+        out_pool = ctx.enter_context(tc.tile_pool(name="result", bufs=6))
         psum = ctx.enter_context(tc.psum_pool(name="psum", bufs=8))
 
         def kept(shape, dtype, name):
@@ -42,6 +42,7 @@ def tile_list_oil_feed_scores_kernel(tc, tab_words, tab_scales, offs, xs_words, 
         tab_w = [kept([P, T], U32, "tab_w%d" % a) for a in range(2)]
         tab_s = kept([P, T], U8, "tab_s")
         v_w = [kept([P, S], U32, "v_w%d" % a) for a in range(2)]
+        v_s_rows = kept([P, S], U8, "v_s_rows")
         v_s = kept([P, S], U8, "v_s")
         xs_w = kept([P, S], U32, "xs_w")
         xs_s = kept([P, S], U8, "xs_s")
@@ -61,6 +62,7 @@ def tile_list_oil_feed_scores_kernel(tc, tab_words, tab_scales, offs, xs_words, 
         h_w = {(b, g): kept([P, HALF], U32, "h_w%d%d" % (b, g)) for b in range(2) for g in range(2)}
         h_s = {(b, g): kept([P, HALF], U8, "h_s%d%d" % (b, g)) for b in range(2) for g in range(2)}
 
+        gain_rows = [kept([P, 2 * UNIT, PACK], F32, "gain_rows%d" % b) for b in range(2)]
         h_bf = [kept([P, 2 * UNIT * PACK], BF16, "h_bf%d" % i) for i in range(3)]
 
         def load_words(dst, src):
@@ -76,29 +78,49 @@ def tile_list_oil_feed_scores_kernel(tc, tab_words, tab_scales, offs, xs_words, 
             rows = w1[a * KP : (a + 1) * KP, b * KP : (b + 1) * KP]
             nc.sync.dma_start(out=w1_raw[a, b][:], in_=rows.rearrange("(p j) c -> p j c", j=PACK))
 
-        nc.vector.memset(tab_s[:].bitcast(I32), 0)
+        def load_w3(b):
+            nc.sync.dma_start(out=w3_raw[b][:], in_=w3[b * KP : (b + 1) * KP, :].rearrange("(p j) c -> p j c", j=PACK))
+
+        def load_table_half(a, half):
+            cols = slice(half * T // 2, (half + 1) * T // 2)
+            load_words(tab_w[a][:, cols], tab_words[a, :, cols, :])
+
+        def move_scale_rows(a, r):
+            nc.sync.dma_start(out=v_s[4 * a + r : P : 32, :].bitcast(I32),
+                              in_=v_s_rows[16 * a + r : 16 * (a + 1) : 4, :].bitcast(I32))
+
+        nc.vector.memset(tab_s[32:64, :].bitcast(I32), 0)
+        nc.vector.memset(tab_s[64:P, :].bitcast(I32), 0)
+        nc.vector.memset(v_s[:].bitcast(I32), 0)
         nc.vector.memset(w2_s_raw[:].bitcast(I32), 0)
         nc.vector.memset(xs_s[:].bitcast(I32), 0)
         nc.vector.memset(w4_s[:].bitcast(I32), 0)
 
-        load_scales(nc.gpsimd, tab_s, tab_scales)
-        nc.gpsimd.dma_start(out=gains[:], in_=gain.rearrange("(b p t) -> p b t", b=2, t=PACK))
-
+        nc.sync.dma_start(out=tab_s[0:32, :].bitcast(I32), in_=tab_scales.rearrange("a q n -> (a q) n").bitcast(I32))
         nc.sync.dma_start(offsets[:], offs)
-        load_words(tab_w[0][:], tab_words[0])
+        nc.vector.tensor_copy(v_s_rows[:], tab_s[:].indirect(offsets[:]))
+        load_table_half(0, 0)
+        nc.sync.dma_start(out=gains[:], in_=gain.rearrange("(b p t) -> p b t", b=2, t=PACK))
+        load_table_half(0, 1)
         nc.sync.dma_start(out=w2_w_raw[:].bitcast(I32), in_=w2_words[0].bitcast(I32))
-        load_scales(nc.sync, w2_s_raw, w2_scales)
         load_w1(0, 0)
-        load_words(xs_w[:], xs_words[0])
+        rows = [(a, r) for a in range(2) for r in range(4)]
+        for a, r in rows[:6]:
+            move_scale_rows(a, r)
+        load_table_half(1, 0)
+        for a, r in rows[6:]:
+            move_scale_rows(a, r)
+        load_scales(nc.sync, w2_s_raw, w2_scales)
+        load_table_half(1, 1)
         load_scales(nc.sync, xs_s, xs_scales)
-        load_words(tab_w[1][:], tab_words[1])
+        load_words(xs_w[:], xs_words[0])
         load_w1(1, 0)
         load_w1(0, 1)
         load_w1(1, 1)
+        load_w3(0)
         nc.sync.dma_start(out=w4_w[:].bitcast(I32), in_=w4_words.rearrange("b p n t -> p b (n t)").bitcast(I32))
         load_scales(nc.sync, w4_s, w4_scales)
-        for b in range(2):
-            nc.sync.dma_start(out=w3_raw[b][:], in_=w3[b * KP : (b + 1) * KP, :].rearrange("(p j) c -> p j c", j=PACK))
+        load_w3(1)
 
         def cast(on_scalar, dst, src):
             if on_scalar:
@@ -113,7 +135,7 @@ def tile_list_oil_feed_scores_kernel(tc, tab_words, tab_scales, offs, xs_words, 
             return (staged, w1_w[a, b][:, t0 * P : t1 * P], w1_s[a, b][:, t0 * P : t1 * P])
 
         def cast_w3(b, c0, c1, on_scalar):
-            staged = cast_pool.tile([P, (c1 - c0) * PACK], BF16, name="staged", align_bytes=64)
+            staged = kept([P, (c1 - c0) * PACK], BF16, "w3_staged%d_%d" % (b, c0))
             src = w3_raw[b][:, :, c0:c1].rearrange("p j (c i) -> p c j i", i=4)
             cast(on_scalar, staged[:].rearrange("p (c i j) -> p c j i", i=4, j=PACK), src)
             return (staged, w3_w[b][:, c0:c1], w3_s[b][:, c0:c1])
@@ -143,13 +165,14 @@ def tile_list_oil_feed_scores_kernel(tc, tab_words, tab_scales, offs, xs_words, 
                     start=start and t == 0, stop=stop and t == PACK - 1)
 
         units = list(range(S // UNIT))
+        for b in range(2):
+            nc.vector.tensor_copy(out=gain_rows[b][:], in_=gains[:, b : b + 1, :].broadcast_to([P, 2 * UNIT, PACK]))
         nc.vector.tensor_copy(v_w[0][:], tab_w[0][:].indirect(offsets[:]))
+        quantize(cast_w1(0, 0, 0, 4, True))
         nc.vector.tensor_copy(out=w2_w[:].rearrange("p (b t m e) -> p b t m e", b=2, t=PACK, e=2),
                               in_=w2_w_raw[:].rearrange("p (b m t e) -> p b t m e", b=2, t=PACK, e=2))
         nc.vector.tensor_copy(out=w2_s[:].rearrange("p (b t m) -> p b t m", b=2, t=PACK),
                               in_=w2_s_raw[:].rearrange("p (b m t) -> p b t m", b=2, t=PACK))
-        nc.vector.tensor_copy(v_s[:], tab_s[:].indirect(offsets[:]))
-        quantize(cast_w1(0, 0, 0, 4, True))
         nc.vector.tensor_copy(v_w[1][:], tab_w[1][:].indirect(offsets[:]))
         low = cast_w1(1, 0, 0, 2, True)
         high = cast_w1(1, 0, 2, 4, False)
@@ -169,9 +192,9 @@ def tile_list_oil_feed_scores_kernel(tc, tab_words, tab_scales, offs, xs_words, 
         def first_hidden_half():
             banks = [psum.tile([P, PACK * UNIT], F32, name="bank") for u in units]
             for u in units:
-                stream_pass(banks[u], 0, u, True, False)
+                table_pass(banks[u], 0, 0, u, True, False)
             for u in units:
-                table_pass(banks[u], 0, 0, u, False, False)
+                stream_pass(banks[u], 0, u, False, False)
             for u in units:
                 table_pass(banks[u], 1, 0, u, False, True)
                 squash(banks[u], 0, u)
@@ -187,7 +210,7 @@ def tile_list_oil_feed_scores_kernel(tc, tab_words, tab_scales, offs, xs_words, 
         def apply_gain(b, pair, h):
             nc.vector.tensor_tensor(out=h[:].rearrange("p (n t) -> p n t", t=PACK),
                                     in0=tanhs[b, pair][:].rearrange("p u n t -> p (u n) t"),
-                                    in1=gains[:, b : b + 1, :].broadcast_to([P, 2 * UNIT, PACK]), op=MULT)
+                                    in1=gain_rows[b][:], op=MULT)
             g, cols = pair // 2, slice((pair % 2) * 2 * UNIT, (pair % 2 + 1) * 2 * UNIT)
             return (h, h_w[b, g][:, cols], h_s[b, g][:, cols])
 
@@ -243,7 +266,7 @@ def tile_list_oil_feed_scores_kernel(tc, tab_words, tab_scales, offs, xs_words, 
                     pending = job
             if g == 1:
                 quantize(pending)
-        w3_jobs = [cast_w3(b, c0, c0 + 256, b == 0 and c0 == 0) for b in range(2) for c0 in (0, 256)]
+        w3_jobs = [cast_w3(0, c0, c0 + 128, True) for c0 in range(0, N, 128)] + [cast_w3(1, 0, N, False)]
         for job in w3_jobs:
             quantize(job)
         factors[0] = damping(0)

from contextlib import ExitStack

import concourse.mybir as mybir

T, S, K, K2, H, N = 4096, 1024, 1024, 512, 1024, 512
FLOPS = 2 * S * (K * H + K2 * H + 2 * H * N)

F32 = mybir.dt.float32
BF16 = mybir.dt.bfloat16
I32 = mybir.dt.int32
U32 = mybir.dt.uint32
U16 = mybir.dt.uint16
U8 = mybir.dt.uint8
FP8X4 = mybir.dt.float8_e4m3fn_x4
FP4X4 = mybir.dt.float4_e2m1fn_x4
ACT = mybir.ActivationFunctionType
MULT = mybir.AluOpType.mult

P = 128
PACK = 4
KP = P * PACK
UNIT = 128
HALF = 512


def tile_list_oil_feed_scores_kernel(tc, tab_words, tab_scales, offs, xs_words, xs_scales, w1, w2_words,
                                               w2_scales, gain, w3, w4_words, w4_scales, out):
    nc = tc.nc
    with ExitStack() as ctx:
        keep = ctx.enter_context(tc.tile_pool(name="keep", bufs=1))
        cast_pool = ctx.enter_context(tc.tile_pool(name="cast", bufs=3))
        tanh_pool = ctx.enter_context(tc.tile_pool(name="tanh", bufs=8))
        sq_pool = ctx.enter_context(tc.tile_pool(name="sq", bufs=4))
        damp_pool = ctx.enter_context(tc.tile_pool(name="damping", bufs=8))
        out_pool = ctx.enter_context(tc.tile_pool(name="result", bufs=6))
        psum = ctx.enter_context(tc.psum_pool(name="psum", bufs=8))

        def kept(shape, dtype, name):
            return keep.tile(shape, dtype, name=name, align_bytes=64)

        offsets = keep.tile([P, S // 16], U16, name="offsets")
        tab_w = [kept([P, T], U32, "tab_w%d" % a) for a in range(2)]
        tab_s = kept([P, T], U8, "tab_s")
        v_w = [kept([P, S], U32, "v_w%d" % a) for a in range(2)]
        v_s_rows = kept([P, S], U8, "v_s_rows")
        v_s = kept([P, S], U8, "v_s")
        xs_w = kept([P, S], U32, "xs_w")
        xs_s = kept([P, S], U8, "xs_s")
        w2_w_raw = kept([P, 2 * H], U8, "w2_w_raw")
        w2_s_raw = kept([P, H], U8, "w2_s_raw")
        w2_w = kept([P, 2 * H], U8, "w2_w")
        w2_s = kept([P, H], U8, "w2_s")
        w4_w = kept([P, 2, N], U32, "w4_w")
        w4_s = kept([P, N], U8, "w4_s")
        gains = kept([P, 2, PACK], F32, "gains")
        w1_raw = {(a, b): kept([P, PACK, KP], F32, "w1_raw%d%d" % (a, b)) for a in range(2) for b in range(2)}
        w1_w = {(a, b): kept([P, KP], U32, "w1_w%d%d" % (a, b)) for a in range(2) for b in range(2)}
        w1_s = {(a, b): kept([P, KP], U8, "w1_s%d%d" % (a, b)) for a in range(2) for b in range(2)}
        w3_raw = [kept([P, PACK, N], F32, "w3_raw%d" % b) for b in range(2)]
        w3_w = [kept([P, N], U32, "w3_w%d" % b) for b in range(2)]
        w3_s = [kept([P, N], U8, "w3_s%d" % b) for b in range(2)]
        h_w = {(b, g): kept([P, HALF], U32, "h_w%d%d" % (b, g)) for b in range(2) for g in range(2)}
        h_s = {(b, g): kept([P, HALF], U8, "h_s%d%d" % (b, g)) for b in range(2) for g in range(2)}

        gain_rows = [kept([P, 2 * UNIT, PACK], F32, "gain_rows%d" % b) for b in range(2)]
        h_bf = [kept([P, 2 * UNIT * PACK], BF16, "h_bf%d" % i) for i in range(3)]

        def load_words(dst, src):
            nc.sync.dma_start(out=dst.bitcast(I32), in_=src.rearrange("p n t -> p (n t)").bitcast(I32))

        def load_scales(queue, dst, src):
            rows = 4 * src.shape[0]
            for q in range(4):
                queue.dma_start(out=dst[32 * q : 32 * q + rows, :].bitcast(I32),
                                in_=src[:, 4 * q : 4 * q + 4, :].bitcast(I32))

        def load_w1(a, b):
            rows = w1[a * KP : (a + 1) * KP, b * KP : (b + 1) * KP]
            nc.sync.dma_start(out=w1_raw[a, b][:], in_=rows.rearrange("(p j) c -> p j c", j=PACK))

        def load_w3(b):
            nc.sync.dma_start(out=w3_raw[b][:], in_=w3[b * KP : (b + 1) * KP, :].rearrange("(p j) c -> p j c", j=PACK))

        def load_table_half(a, half):
            cols = slice(half * T // 2, (half + 1) * T // 2)
            load_words(tab_w[a][:, cols], tab_words[a, :, cols, :])

        def move_scale_rows(a, r):
            nc.sync.dma_start(out=v_s[4 * a + r : P : 32, :].bitcast(I32),
                              in_=v_s_rows[16 * a + r : 16 * (a + 1) : 4, :].bitcast(I32))

        nc.vector.memset(tab_s[32:64, :].bitcast(I32), 0)
        nc.vector.memset(tab_s[64:P, :].bitcast(I32), 0)
        nc.vector.memset(v_s[:].bitcast(I32), 0)
        nc.vector.memset(w2_s_raw[:].bitcast(I32), 0)
        nc.vector.memset(xs_s[:].bitcast(I32), 0)
        nc.vector.memset(w4_s[:].bitcast(I32), 0)

        nc.sync.dma_start(out=tab_s[0:32, :].bitcast(I32), in_=tab_scales.rearrange("a q n -> (a q) n").bitcast(I32))
        nc.sync.dma_start(offsets[:], offs)
        nc.vector.tensor_copy(v_s_rows[:], tab_s[:].indirect(offsets[:]))
        load_table_half(0, 0)
        nc.sync.dma_start(out=gains[:], in_=gain.rearrange("(b p t) -> p b t", b=2, t=PACK))
        load_table_half(0, 1)
        nc.sync.dma_start(out=w2_w_raw[:].bitcast(I32), in_=w2_words[0].bitcast(I32))
        load_w1(0, 0)
        rows = [(a, r) for a in range(2) for r in range(4)]
        for a, r in rows[:6]:
            move_scale_rows(a, r)
        load_table_half(1, 0)
        for a, r in rows[6:]:
            move_scale_rows(a, r)
        load_scales(nc.sync, w2_s_raw, w2_scales)
        load_table_half(1, 1)
        load_scales(nc.sync, xs_s, xs_scales)
        load_words(xs_w[:], xs_words[0])
        load_w1(1, 0)
        load_w1(0, 1)
        load_w1(1, 1)
        load_w3(0)
        nc.sync.dma_start(out=w4_w[:].bitcast(I32), in_=w4_words.rearrange("b p n t -> p b (n t)").bitcast(I32))
        load_scales(nc.sync, w4_s, w4_scales)
        load_w3(1)

        def cast(on_scalar, dst, src):
            if on_scalar:
                nc.scalar.activation(out=dst, in_=src, func=ACT.Copy)
            else:
                nc.vector.tensor_copy(out=dst, in_=src)

        def cast_w1(a, b, t0, t1, on_scalar):
            staged = cast_pool.tile([P, (t1 - t0) * KP], BF16, name="staged", align_bytes=64)
            src = w1_raw[a, b][:].rearrange("p j (m t) -> p m j t", t=PACK)[:, :, :, t0:t1]
            cast(on_scalar, staged[:].rearrange("p (t m j) -> p m j t", m=P, j=PACK), src)
            return (staged, w1_w[a, b][:, t0 * P : t1 * P], w1_s[a, b][:, t0 * P : t1 * P])

        def cast_w3(b, c0, c1, on_scalar):
            staged = kept([P, (c1 - c0) * PACK], BF16, "w3_staged%d_%d" % (b, c0))
            src = w3_raw[b][:, :, c0:c1].rearrange("p j (c i) -> p c j i", i=4)
            cast(on_scalar, staged[:].rearrange("p (c i j) -> p c j i", i=4, j=PACK), src)
            return (staged, w3_w[b][:, c0:c1], w3_s[b][:, c0:c1])

        def quantize(job):
            staged, words, scales = job
            nc.vector.quantize_mx(out=words.bitcast(FP8X4), scales=scales, in_=staged[:])

        def stream_pass(bank, b, u, start, stop):
            cols = slice(u * UNIT, (u + 1) * UNIT)
            for t in range(PACK):
                c0 = b * KP + t * P
                nc.tensor.matmul_mx(
                    out=bank[:, t * UNIT : (t + 1) * UNIT],
                    lhsT=w2_w[:, 2 * c0 : 2 * (c0 + P)].bitcast(FP4X4), lhsT_scale=w2_s[:, c0 : c0 + P],
                    rhs=xs_w[:, cols].bitcast(FP8X4), rhs_scale=xs_s[:, cols],
                    start=start and t == 0, stop=stop and t == PACK - 1)

        def table_pass(bank, a, b, u, start, stop):
            cols = slice(u * UNIT, (u + 1) * UNIT)
            for t in range(PACK):
                wcols = slice(t * P, (t + 1) * P)
                nc.tensor.matmul_mx(
                    out=bank[:, t * UNIT : (t + 1) * UNIT],
                    lhsT=w1_w[a, b][:, wcols].bitcast(FP8X4), lhsT_scale=w1_s[a, b][:, wcols],
                    rhs=v_w[a][:, cols].bitcast(FP8X4), rhs_scale=v_s[4 * a : P, cols],
                    start=start and t == 0, stop=stop and t == PACK - 1)

        units = list(range(S // UNIT))
        for b in range(2):
            nc.vector.tensor_copy(out=gain_rows[b][:], in_=gains[:, b : b + 1, :].broadcast_to([P, 2 * UNIT, PACK]))
        nc.vector.tensor_copy(v_w[0][:], tab_w[0][:].indirect(offsets[:]))
        quantize(cast_w1(0, 0, 0, 4, True))
        nc.vector.tensor_copy(out=w2_w[:].rearrange("p (b t m e) -> p b t m e", b=2, t=PACK, e=2),
                              in_=w2_w_raw[:].rearrange("p (b m t e) -> p b t m e", b=2, t=PACK, e=2))
        nc.vector.tensor_copy(out=w2_s[:].rearrange("p (b t m) -> p b t m", b=2, t=PACK),
                              in_=w2_s_raw[:].rearrange("p (b m t) -> p b t m", b=2, t=PACK))
        nc.vector.tensor_copy(v_w[1][:], tab_w[1][:].indirect(offsets[:]))
        low = cast_w1(1, 0, 0, 2, True)
        high = cast_w1(1, 0, 2, 4, False)
        quantize(high)
        quantize(low)
        quantize(cast_w1(0, 1, 0, 4, False))
        quantize(cast_w1(1, 1, 0, 4, False))

        tanhs = {}

        def squash(bank, b, u):
            if u % 2 == 0:
                tanhs[b, u // 2] = tanh_pool.tile([P, 2, UNIT, PACK], F32, name="tanh")
            nc.scalar.activation(out=tanhs[b, u // 2][:, u % 2, :, :],
                                 in_=bank[:].rearrange("p (t n) -> p n t", t=PACK), func=ACT.Tanh)

        def first_hidden_half():
            banks = [psum.tile([P, PACK * UNIT], F32, name="bank") for u in units]
            for u in units:
                table_pass(banks[u], 0, 0, u, True, False)
            for u in units:
                stream_pass(banks[u], 0, u, False, False)
            for u in units:
                table_pass(banks[u], 1, 0, u, False, True)
                squash(banks[u], 0, u)

        def second_hidden_half():
            for u in units:
                bank = psum.tile([P, PACK * UNIT], F32, name="bank")
                stream_pass(bank, 1, u, True, False)
                table_pass(bank, 0, 1, u, False, False)
                table_pass(bank, 1, 1, u, False, True)
                squash(bank, 1, u)

        def apply_gain(b, pair, h):
            nc.vector.tensor_tensor(out=h[:].rearrange("p (n t) -> p n t", t=PACK),
                                    in0=tanhs[b, pair][:].rearrange("p u n t -> p (u n) t"),
                                    in1=gain_rows[b][:], op=MULT)
            g, cols = pair // 2, slice((pair % 2) * 2 * UNIT, (pair % 2 + 1) * 2 * UNIT)
            return (h, h_w[b, g][:, cols], h_s[b, g][:, cols])

        def readout(words, scales, g):
            banks = []
            for i in range(N // P):
                bank = psum.tile([P, HALF], F32, name="bank")
                cols = slice(i * P, (i + 1) * P)
                for b in range(2):
                    nc.tensor.matmul_mx(
                        out=bank[:], lhsT=words(b, cols).bitcast(FP8X4), lhsT_scale=scales(b, cols),
                        rhs=h_w[b, g][:].bitcast(FP8X4), rhs_scale=h_s[b, g][:], start=b == 0, stop=b == 1)
                banks.append(bank)
            return banks

        def pieces(g, i):
            last = g == 1 and i == N // P - 1
            return [slice(0, HALF // 2), slice(HALF // 2, HALF)] if last else [slice(0, HALF)]

        def damping(g):
            banks = readout(lambda b, cols: w4_w[:, b, cols], lambda b, cols: w4_s[4 * b : P, cols], g)
            factors = []
            for i, bank in enumerate(banks):
                square = sq_pool.tile([P, HALF], F32, name="square")
                factor = damp_pool.tile([P, HALF], F32, name="factor")
                for cols in pieces(g, i):
                    nc.scalar.activation(out=square[:, cols], in_=bank[:, cols], func=ACT.Square)
                for cols in pieces(g, i):
                    nc.scalar.activation(out=factor[:, cols], in_=square[:, cols], func=ACT.Abs_reciprocal_sqrt,
                                         bias=1.0)
                factors.append(factor)
            return factors

        def feed(g, factors):
            banks = readout(lambda b, cols: w3_w[b][:, cols], lambda b, cols: w3_s[b][:, cols], g)
            for i, bank in enumerate(banks):
                result = out_pool.tile([P, HALF], F32, name="result")
                rows = out[i * P : (i + 1) * P, g * HALF : (g + 1) * HALF]
                for cols in pieces(g, i):
                    nc.vector.tensor_tensor(out=result[:, cols], in0=bank[:, cols], in1=factors[i][:, cols], op=MULT)
                    nc.sync.dma_start(out=rows[:, cols], in_=result[:, cols])

        first_hidden_half()
        second_hidden_half()
        pending = None
        factors = {}
        for g in range(2):
            for b in range(2):
                for pair in (2 * g, 2 * g + 1):
                    job = apply_gain(b, pair, h_bf[(4 * g + 2 * b + pair % 2) % 3])
                    if pending is not None:
                        quantize(pending)
                    pending = job
            if g == 1:
                quantize(pending)
        w3_jobs = [cast_w3(0, c0, c0 + 128, True) for c0 in range(0, N, 128)] + [cast_w3(1, 0, N, False)]
        for job in w3_jobs:
            quantize(job)
        factors[0] = damping(0)
        factors[1] = damping(1)
        feed(0, factors[0])
        feed(1, factors[1])
